import numpy as np, ml_dtypes
CORES = [2,3,42,43,82,83,122,123]
N = 8
import mx_ref
BF = ml_dtypes.bfloat16
def entries(a):
    return np.ascontiguousarray(a.T).reshape(-1)
def table(e):
    return np.ascontiguousarray(np.reshape(e, (-1, 16)).T).astype(np.int32)
def cols(t, e):
    v = np.concatenate([t.reshape(128, -1, 4), np.zeros((128, 1, 4), BF)], axis=1)
    return np.ascontiguousarray(v[:, e]).reshape(128, -1)
def f(rng, *shape):
    return mx_ref.flush((rng.standard_normal(shape, dtype=np.float32) * np.exp2(rng.integers(-2, 3, shape[:-1] + (1,)))).astype(BF))
def wide(rng, *shape, cols=0):
    v = rng.standard_normal(shape, dtype=np.float32) * np.exp2(rng.integers(-12, 13, shape)).astype(np.float32)
    if cols: v *= np.repeat(np.exp2(rng.integers(-cols, cols + 1, shape[:-2] + (1, shape[-1] // 4))) * (rng.random(shape[:-2] + (1, shape[-1] // 4)) > 0.0625), 4, axis=-1).astype(np.float32)
    return mx_ref.flush(v.astype(BF))
T, CAPP = 256, 48
def even(n):
    return [T // n + (k < T % n) for k in range(n)]
def counts(rng, h, moves=10 * N * N):
    n = np.array([[h[(d - s) % N] for d in range(N)] for s in range(N)])[rng.permutation(N)][:, rng.permutation(N)]
    top = np.where(n > 0, CAPP, 0)
    for _ in range(moves):
        a, b = rng.permutation(N)[:2]; c, e = rng.permutation(N)[:2]
        k = rng.integers(0, min(n[a, e], n[b, c], top[a, c] - n[a, c], top[b, e] - n[b, e]) + 1)
        n[a, c] += k; n[b, e] += k; n[a, e] -= k; n[b, c] -= k
    return n
def lists(rng, n, back=False):
    a = np.full((N, N, CAPP), -1)
    for s in range(N):
        p = np.arange(T)[::-1] if back else rng.permutation(T)
        for d in range(N):
            k = rng.permutation(CAPP)[:n[s, d]]
            if back: k = np.sort(k)
            a[s, d, k] = p[:n[s, d]]; p = p[n[s, d]:]
    m = []
    for d in range(N):
        k = np.flatnonzero(a[:, d].reshape(-1) >= 0)
        m.append(table(k[::-1] if back else rng.permutation(k)))
    return {"send": np.stack([table(a[s].reshape(-1)) for s in range(N)]), "mine": np.stack(m), "prev": np.stack([m[(r - 1) % N] for r in range(N)])}
def setup_inputs(rng):
    return {"x": f(rng, N, 128, 4 * T), **lists(rng, counts(rng, even(N)))}
def setup_inputs_empty(rng):
    return {**setup_inputs(rng), **lists(rng, counts(rng, even(N - 1) + [0]))}
def setup_inputs_full(rng):
    return {**setup_inputs(rng), **lists(rng, counts(rng, [min(CAPP, max(0, T - k * CAPP)) for k in range(N)], 0))}
def setup_inputs_reversed(rng):
    return {**setup_inputs(rng), **lists(rng, counts(rng, even(N)), back=True)}
def setup_inputs_spread(rng):
    d = setup_inputs(rng); d["x"] = wide(rng, N, 128, 4 * T, cols=8); return d
def check_inputs(d):
    b = []
    v = np.abs(np.asarray(d["x"]).astype(np.float32))
    if not ((v == 0) | ((v >= 2.0 ** -30) & (v <= 2.0 ** 30))).all(): b.append("x")
    for r in range(N):
        c, m = entries(d["send"][r]), entries(d["mine"][r])
        if c.min() < -1 or not np.array_equal(np.sort(c[c >= 0]), np.arange(T)): b.append("send")
        arrived = np.concatenate([entries(d["send"][s])[r * CAPP:(r + 1) * CAPP] for s in range(N)])
        if not np.array_equal(np.sort(m), np.flatnonzero(arrived >= 0)): b.append("mine")
        if not np.array_equal(d["prev"][r], d["mine"][(r - 1) % N]): b.append("prev")
    return b
def reference(x, send, mine, prev):
    K = []
    for r in range(N):
        arrived = np.concatenate([cols(x[s], entries(send[s])[r * CAPP:(r + 1) * CAPP]) for s in range(N)], axis=1)
        K.append(cols(arrived, entries(mine[r])))
    Q = [mx_ref.quantize(t) for t in K]
    y = np.zeros((N, T, 2 * T), np.float32)
    for r in range(N):
        for p in range(T // 128):
            W = mx_ref.quantize(np.ascontiguousarray(K[r][:, 512 * p:512 * p + 512]))
            y[r, 128 * p:128 * p + 128, :T] = mx_ref.matmul(W, Q[r])
            y[r, 128 * p:128 * p + 128, T:] = mx_ref.matmul(W, Q[(r - 1) % N])
    return {"y": y}

@@ -1,0 +1,246 @@
+from concourse.bass import DstId, RemoteDMATransfer, IndirectOffsetOnAxis
+from concourse.mybir import dt, AluOpType, AxisListType, ActivationFunctionType
+
+N, NT, CAPP = 8, 256, 48
+HALF = N // 2 * CAPP
+ARR = N * CAPP
+W16 = CAPP // 16
+NTILE = ARR // 128
+SKIP = 1000.0
+
+SCRATCH = {
+    "xs": ("sbuf", [128, 4 * NT], "bfloat16"),
+    "lsend": ("sbuf", [128, N * W16], "int32"),
+    "lmine": ("sbuf", [128, NT // 16], "int32"),
+    "lprev": ("sbuf", [128, NT // 16], "int32"),
+    "offa": ("sbuf", [128, HALF // 16], "uint16"),
+    "offb": ("sbuf", [128, HALF // 16], "uint16"),
+    "moff": ("sbuf", [128, NT // 16], "uint16"),
+    "poff": ("sbuf", [128, NT // 16], "uint16"),
+    "ha": ("sbuf", [128, 4 * HALF], "bfloat16"),
+    "hb": ("sbuf", [128, 4 * HALF], "bfloat16"),
+    "qa_c": ("sbuf", [128, HALF], "float8_e4m3fn_x4"),
+    "qa_s": ("sbuf", [128, HALF], "uint8"),
+    "qb_c": ("sbuf", [128, HALF], "float8_e4m3fn_x4"),
+    "qb_s": ("sbuf", [128, HALF], "uint8"),
+    "own_c": ("sbuf", [128, ARR], "float8_e4m3fn_x4"),
+    "own_s": ("sbuf", [128, ARR], "uint8"),
+    "prv_c": ("sbuf", [128, ARR], "float8_e4m3fn_x4"),
+    "prv_s": ("sbuf", [128, ARR], "uint8"),
+    "places": ("sbuf", [128, NT], "float32"),
+    "pcol": ("sbuf", [128, 4], "float32"),
+    "diag": ("sbuf", [128, 128], "float32"),
+    "inv": ("sbuf", [128, ARR], "float32"),
+    "pick": ("sbuf", [128, ARR], "float32"),
+    "idxf": ("sbuf", [128, 4], "float32"),
+    "idx": ("sbuf", [128, 4], "int32"),
+    "ps": ("psum", [128, 512 * 2 * NTILE], "float32"),
+}
+for _t in range(NTILE):
+    SCRATCH["raw%d" % _t] = ("sbuf", [128, 2 * ARR], "float32")
+    SCRATCH["row%d" % _t] = ("sbuf", [128, 2 * NT], "float32")
+
+SEMAPHORES = ["ld_send", "ld_x", "ld_mine", "ld_prev", "ld_g", "iot", "inv0", "cva", "cvb", "ga", "gb", "qa", "qb",
+              "selfc", "own_in", "prv_in", "sent", "mo", "po", "invd", "dia", "pk", "ixf", "ix"]
+for _t in range(NTILE):
+    SEMAPHORES += ["peo%d" % _t, "pep%d" % _t, "evo%d" % _t, "evp%d" % _t, "rw%d" % _t, "st%d" % _t]
+
+
+def rank_program(g, core, T, topo):
+    rank = T.rank_of(core)
+    if rank is None:
+        return
+    V, S, Y, P, M = g.vector, g.scalar, g.sync, g.tensor, T.sem
+    COPY = ActivationFunctionType.Copy
+    cores = list(T.cores)
+    chip = [topo.chip(c) for c in cores]
+    here = chip[rank]
+    sib = [r for r in range(N) if r != rank and chip[r] == here][0]
+    shared = [d for d in range(N) if chip[d] == chip[(d + 1) % N]]
+    rest = [d for d in range(N) if d not in shared]
+    before = (rank - 1) % N
+    heads = before not in shared
+    away = [r for r in range(N) if chip[r] != here]
+    off = topo.engines(core, cores[away[0]])
+    near = [e for e in topo.engines(core, cores[sib]) if e not in off]
+
+    def bits(es):
+        m = 0
+        for e in es:
+            m |= 1 << e
+        return m
+
+    EA, EB, EF = 2, 1, 2
+
+    def transfer(dst, es, sem, src, out):
+        rid, pid = topo.addr(cores[dst])[:2]
+        return RemoteDMATransfer(dst_ids=[DstId(rid=rid, pnc=pid)], dma_engine_mask=bits(es), remote_sem=sem,
+                                 src=src, dst=out)
+
+    def both(moves, slot):
+        for kind in ("_c", "_s"):
+            ts = []
+            for dst, es, sem, a, i, b, j, w in moves:
+                src, out = T[a + kind][:, i:i + w], T[b + kind][:, j:j + w]
+                if kind == "_c":
+                    src, out = src.bitcast(dt.uint8), out.bitcast(dt.uint8)
+                ts.append(transfer(dst, es, sem, src, out))
+            g.remote_dma_fused(ts, local_sem=M.sent)
+        return 2 * sum(len(m[1]) for m in moves)
+
+    def at(d):
+        return (shared if d in shared else rest).index(d) * CAPP
+
+    for k in range(5):
+        S.dma_start(T.lsend[16 * k:16 * k + 16, :], T.send[:]).then_inc(M.ld_send, 16)
+    for k in range(5, 8):
+        Y.dma_start(T.lsend[16 * k:16 * k + 16, :], T.send[:]).then_inc(M.ld_send, 16)
+    Y.dma_start(T.xs[:], T.x[:]).then_inc(M.ld_x, 16)
+    g.dma_start(T.lmine[0:16, :], T.mine[:]).then_inc(M.ld_g, 16)
+    for k in range(1, 8):
+        Y.dma_start(T.lmine[16 * k:16 * k + 16, :], T.mine[:]).then_inc(M.ld_mine, 16)
+    for k in range(8):
+        Y.dma_start(T.lprev[16 * k:16 * k + 16, :], T.prev[:]).then_inc(M.ld_prev, 16)
+    g.iota(T.places[:], [[1, NT]], 0, 0, allow_small_or_imprecise_dtypes=True).then_inc(M.iot, 1)
+    g.iota(T.pcol[:], [[0, 4]], 0, 1, allow_small_or_imprecise_dtypes=True).then_inc(M.iot, 1)
+    V.memset(T.inv[:], SKIP).then_inc(M.inv0, 1)
+
+    V.wait_ge(M.ld_send, 128)
+    for buf, sem, first in (("offa", M.cva, shared[0]), ("offb", M.cvb, rest[0])):
+        for w in range(W16):
+            V.tensor_scalar(T[buf][:, w:HALF // 16:W16], T.lsend[:, W16 * first + w:N * W16:2 * W16], 0, 4,
+                            AluOpType.max, AluOpType.mult).then_inc(sem, 1)
+
+    def gather(eng, tile, offs, t, sem):
+        win = T.xs[:, t:4 * NT].indirect(T[offs][:, 0:HALF // 16])
+        if eng is V:
+            V.tensor_copy(T[tile][:, t:4 * HALF:4], win).then_inc(sem, 1)
+        else:
+            S.activation(T[tile][:, t:4 * HALF:4], win, COPY).then_inc(sem, 1)
+
+    for eng in (V, S):
+        eng.wait_ge(M.ld_x, 16)
+        eng.wait_ge(M.cva, W16)
+    for eng, t in ((V, 0), (S, 2), (V, 1), (S, 3)):
+        gather(eng, "ha", "offa", t, M.ga)
+    for eng in (V, S):
+        eng.wait_ge(M.cvb, W16)
+    for t in (2, 3):
+        gather(S, "hb", "offb", t, M.gb)
+    V.wait_ge(M.ga, 4)
+    V.quantize_mx(T.qa_c[:], T.qa_s[:], T.ha[:]).then_inc(M.qa, 1)
+    for t in (0, 1):
+        gather(V, "hb", "offb", t, M.gb)
+    V.wait_ge(M.gb, 4)
+    V.quantize_mx(T.qb_c[:], T.qb_s[:], T.hb[:]).then_inc(M.qb, 1)
+
+    sent = 0
+    mine_sl = rank * CAPP
+    hops = []
+    for k, r in enumerate([r for r in away if r in shared]):
+        es = ([off[4], off[5]], [off[6], off[7]], [off[0], off[2]])[k]
+        hops.append((r, es, M.own_in, "qa", at(r), "own", mine_sl, CAPP))
+    b = rank if heads else before
+    hops.append((sib, [off[1], off[3]], M.prv_in if heads else M.own_in, "qa", at(b), "prv" if heads else "own",
+                 mine_sl, CAPP))
+    g.wait_ge(M.qa, 1)
+    sent += both(hops, mine_sl)
+    hops = []
+    lone = [off[0], off[1], off[2], off[3], off[4], off[6]]
+    for d in rest:
+        for r, sem, buf in ((d, M.own_in, "own"), ((d + 1) % N, M.prv_in, "prv")):
+            if chip[r] != here:
+                hops.append((r, [lone.pop(0)], sem, "qb", at(d), buf, mine_sl, CAPP))
+            elif r == sib:
+                hops.append((r, [off[5]], sem, "qb", at(d), buf, mine_sl, CAPP))
+    g.wait_ge(M.qb, 1)
+    sent += both(hops, mine_sl)
+
+    for d, buf in ((rank, "own"), (before, "prv")):
+        q, sem = ("qa", M.qa) if d in shared else ("qb", M.qb)
+        Y.wait_ge(sem, 1)
+        Y.dma_start(T[buf + "_c"][:, mine_sl:mine_sl + CAPP].bitcast(dt.uint8),
+                    T[q + "_c"][:, at(d):at(d) + CAPP].bitcast(dt.uint8)).then_inc(M.selfc, 16)
+        Y.dma_start(T[buf + "_s"][:, mine_sl:mine_sl + CAPP], T[q + "_s"][:, at(d):at(d) + CAPP]).then_inc(M.selfc, 16)
+
+    chips = sorted(set(chip[r] for r in away), key=lambda c: chip.index(c))
+    if heads:
+        own_n = 2 * EA * (len(away) + 1)
+        prv_n = 2 * EB * (len(away) + 1)
+    else:
+        own_n = 2 * EB * (len(away) + 1)
+        prv_n = 2 * EA + 2 * EF * len(chips)
+    if heads:
+        hops = []
+        for k, c in enumerate(chips):
+            j = chip.index(c) * CAPP
+            hops.append((sib, near[EF * k:EF * k + EF], M.prv_in, "own", j, "prv", j, 2 * CAPP))
+        g.wait_ge(M.own_in, own_n)
+        sent += both(hops, 0)
+
+    V.wait_ge(M.ld_mine, 112)
+    V.wait_ge(M.ld_g, 16)
+    V.tensor_copy(T.moff[:], T.lmine[:]).then_inc(M.mo, 1)
+    V.wait_ge(M.ld_prev, 128)
+    V.tensor_copy(T.poff[:], T.lprev[:]).then_inc(M.po, 1)
+    V.wait_ge(M.iot, 2)
+    V.tensor_scalar(T.diag[:], T.places[:, 0:128], T.pcol[:, 0:1], None, AluOpType.is_equal).then_inc(M.dia, 1)
+    V.wait_ge(M.mo, 1)
+    V.wait_ge(M.inv0, 1)
+    V.tensor_copy(T.inv[:].indirect(T.moff[:]), T.places[:]).then_inc(M.invd, 1)
+    V.wait_ge(M.invd, 1)
+    V.wait_ge(M.dia, 1)
+    for t in range(NTILE):
+        V.tensor_tensor(T.pick[:, 128 * t:128 * t + 128], T.inv[:, 128 * t:128 * t + 128], T.diag[:],
+                        AluOpType.mult).then_inc(M.pk, 1)
+    V.wait_ge(M.pk, NTILE)
+    for t in range(NTILE):
+        V.tensor_reduce(T.idxf[:, t:t + 1], T.pick[:, 128 * t:128 * t + 128], AxisListType.X,
+                        AluOpType.add).then_inc(M.ixf, 1)
+    V.wait_ge(M.ixf, NTILE)
+    V.tensor_copy(T.idx[:, 0:NTILE], T.idxf[:, 0:NTILE]).then_inc(M.ix, 1)
+
+    P.wait_ge(M.selfc, 64)
+    P.wait_ge(M.own_in, own_n)
+    for side, b0, pe in (("own", 0, "peo"), ("prv", NTILE, "pep")):
+        if side == "prv":
+            P.wait_ge(M.prv_in, prv_n)
+        for t in range(NTILE):
+            c0 = 512 * (b0 + t)
+            P.matmul_mx(T.ps[:, c0:c0 + ARR], T.own_c[:, 128 * t:128 * t + 128], T.own_s[:, 128 * t:128 * t + 128],
+                        T[side + "_c"][:], T[side + "_s"][:], True, True).then_inc(M[pe + str(t)], 1)
+
+    def leave(eng, t, h):
+        c0 = 512 * (h * NTILE + t)
+        out, src, sem = T["raw%d" % t][:, h * ARR:h * ARR + ARR], T.ps[:, c0:c0 + ARR], M["ev%s%d" % ("op"[h], t)]
+        eng.wait_ge(M["pe%s%d" % ("op"[h], t)], 1)
+        if eng is V:
+            V.tensor_copy(out, src).then_inc(sem, 1)
+        else:
+            S.activation(out, src, COPY).then_inc(sem, 1)
+
+    def order(eng, t, h):
+        win = T["raw%d" % t][:, h * ARR:h * ARR + ARR].indirect(T[("moff", "poff")[h]][:])
+        out = T["row%d" % t][:, h * NT:h * NT + NT]
+        eng.wait_ge(M["ev%s%d" % ("op"[h], t)], 1)
+        if eng is V:
+            V.tensor_copy(out, win).then_inc(M["rw%d" % t], 1)
+        else:
+            S.activation(out, win, COPY).then_inc(M["rw%d" % t], 1)
+
+    V.wait_ge(M.po, 1)
+    S.wait_ge(M.mo, 1)
+    S.wait_ge(M.po, 1)
+    leave(V, 0, 0), leave(V, 2, 0), order(V, 0, 0), order(V, 2, 0)
+    leave(S, 1, 0), order(S, 1, 0)
+    leave(V, 0, 1), order(V, 0, 1), leave(V, 2, 1), order(V, 2, 1)
+    leave(S, 1, 1), order(S, 1, 1)
+
+    g.wait_ge(M.ix, 1)
+    for t in range(NTILE):
+        g.wait_ge(M["rw%d" % t], 2)
+        g.indirect_dma_start(T.y[:], IndirectOffsetOnAxis(ap=T.idx[:, t:t + 1], axis=0), T["row%d" % t][:], None,
+                             bounds_check=NT - 1, oob_is_err=False).then_inc(M["st%d" % t], 16)
+    g.wait_ge(M.sent, sent)
+    for t in range(NTILE):
+        g.wait_ge(M["st%d" % t], 16)

@@ -2,27 +2,21 @@ from concourse.bass import DstId, RemoteDMATransfer, IndirectOffsetOnAxis
 from concourse.mybir import dt, AluOpType, AxisListType, ActivationFunctionType
 
 N, NT, CAPP = 8, 256, 48
-HALF = N // 2 * CAPP
 ARR = N * CAPP
+NBUCK = (1, 2, 5)
+WIDTH = (128, 128, 240)
 W16 = CAPP // 16
+L16 = NT // 16
 NTILE = ARR // 128
 SKIP = 1000.0
 
 SCRATCH = {
     "xs": ("sbuf", [128, 4 * NT], "bfloat16"),
     "lsend": ("sbuf", [128, N * W16], "int32"),
-    "lmine": ("sbuf", [128, NT // 16], "int32"),
-    "lprev": ("sbuf", [128, NT // 16], "int32"),
-    "offa": ("sbuf", [128, HALF // 16], "uint16"),
-    "offb": ("sbuf", [128, HALF // 16], "uint16"),
-    "moff": ("sbuf", [128, NT // 16], "uint16"),
-    "poff": ("sbuf", [128, NT // 16], "uint16"),
-    "ha": ("sbuf", [128, 4 * HALF], "bfloat16"),
-    "hb": ("sbuf", [128, 4 * HALF], "bfloat16"),
-    "qa_c": ("sbuf", [128, HALF], "float8_e4m3fn_x4"),
-    "qa_s": ("sbuf", [128, HALF], "uint8"),
-    "qb_c": ("sbuf", [128, HALF], "float8_e4m3fn_x4"),
-    "qb_s": ("sbuf", [128, HALF], "uint8"),
+    "lists": ("sbuf", [128, 2 * L16], "int32"),
+    "wrap": ("sbuf", [128, 2 * L16], "int32"),
+    "turn": ("sbuf", [128, 2 * L16], "int32"),
+    "moff": ("sbuf", [128, 2 * L16], "uint16"),
     "own_c": ("sbuf", [128, ARR], "float8_e4m3fn_x4"),
     "own_s": ("sbuf", [128, ARR], "uint8"),
     "prv_c": ("sbuf", [128, ARR], "float8_e4m3fn_x4"),
@@ -34,15 +28,19 @@ SCRATCH = {
     "pick": ("sbuf", [128, ARR], "float32"),
     "idxf": ("sbuf", [128, 4], "float32"),
     "idx": ("sbuf", [128, 4], "int32"),
-    "ps": ("psum", [128, 512 * 2 * NTILE], "float32"),
+    "ps": ("psum", [128, 512 * (2 * NTILE + 1)], "float32"),
 }
+SEMAPHORES = ["ld_send", "ld_x", "ld_lists", "ld_g", "iot", "inv0", "zero", "selfc", "hand_c", "hand_s", "own_in",
+              "prv_in", "sent", "wr", "tu", "mo", "invd", "dia", "pk", "ixf", "ix", "pepx"]
+for _t in range(3):
+    SCRATCH["off%d" % _t] = ("sbuf", [128, NBUCK[_t] * W16], "uint16")
+    SCRATCH["h%d" % _t] = ("sbuf", [128, 4 * WIDTH[_t]], "bfloat16")
+    SCRATCH["q%d_c" % _t] = ("sbuf", [128, WIDTH[_t]], "float8_e4m3fn_x4")
+    SCRATCH["q%d_s" % _t] = ("sbuf", [128, WIDTH[_t]], "uint8")
+    SEMAPHORES += ["cv%d" % _t, "ga%d" % _t, "q%d" % _t]
 for _t in range(NTILE):
     SCRATCH["raw%d" % _t] = ("sbuf", [128, 2 * ARR], "float32")
     SCRATCH["row%d" % _t] = ("sbuf", [128, 2 * NT], "float32")
-
-SEMAPHORES = ["ld_send", "ld_x", "ld_mine", "ld_prev", "ld_g", "iot", "inv0", "cva", "cvb", "ga", "gb", "qa", "qb",
-              "selfc", "own_in", "prv_in", "sent", "mo", "po", "invd", "dia", "pk", "ixf", "ix"]
-for _t in range(NTILE):
     SEMAPHORES += ["peo%d" % _t, "pep%d" % _t, "evo%d" % _t, "evp%d" % _t, "rw%d" % _t, "st%d" % _t]
 
 
@@ -54,15 +52,70 @@ def rank_program(g, core, T, topo):
     COPY = ActivationFunctionType.Copy
     cores = list(T.cores)
     chip = [topo.chip(c) for c in cores]
-    here = chip[rank]
-    sib = [r for r in range(N) if r != rank and chip[r] == here][0]
     shared = [d for d in range(N) if chip[d] == chip[(d + 1) % N]]
     rest = [d for d in range(N) if d not in shared]
     before = (rank - 1) % N
-    heads = before not in shared
-    away = [r for r in range(N) if chip[r] != here]
-    off = topo.engines(core, cores[away[0]])
-    near = [e for e in topo.engines(core, cores[sib]) if e not in off]
+
+    def head(r):
+        return r if r in shared else r - 1
+
+    def tiles(s):
+        a = sorted([d for d in shared if chip[d] != chip[s]], key=lambda d: (d - s) % N)
+        return a[:1], a[1:], [head(s)] + rest
+
+    def at(s, d):
+        for k, ds in enumerate(tiles(s)):
+            if d in ds:
+                return "q%d" % k, ds.index(d) * CAPP
+
+    def base(r):
+        return (head(r) + 2) % N
+
+    def slot(r, s):
+        return (s - base(r)) % N * CAPP
+
+    def plan(s):
+        away = [r for r in range(N) if chip[r] != chip[s]]
+        sib = [r for r in range(N) if r != s and chip[r] == chip[s]][0]
+        off = topo.engines(cores[s], cores[away[0]])
+        near = [e for e in topo.engines(cores[s], cores[sib]) if e not in off]
+        q = len(off) // 4
+        G = [off[q * k:q * k + q] for k in range(4)]
+
+        def deal(a, b, c, d):
+            return [G[c], G[d], G[a] + G[b]]
+
+        def move(r, d, buf, es, fs, sems=None):
+            return (r, es, fs, sems or (buf + "_in",) * 2) + at(s, d) + (buf, slot(r, s), CAPP)
+
+        hand = ("hand_c", "hand_s")
+        a0, a1, _ = tiles(s)
+        rounds = [[move(a0[0], a0[0], "own", off, off, hand)],
+                  [move(a1[0], a1[0], "own", G[0] + G[1], G[2] + G[3], hand),
+                   move(a1[1], a1[1], "own", G[2] + G[3], G[0] + G[1], hand)], [], [], [], []]
+        for k, step, buf, es, fs in ((2, 0, "own", deal(0, 1, 2, 3), deal(2, 3, 0, 1)),
+                                     (3, 1, "prv", deal(2, 3, 0, 1), deal(0, 1, 2, 3))):
+            for d in rest:
+                r = (d + step) % N
+                if r in away:
+                    rounds[k].append(move(r, d, buf, es.pop(0), fs.pop(0)))
+        w, h = len(near) // 4, len(near) // 2
+        pairs = ([(s, "prv"), (sib, "own")] if s in shared else [(sib, "own"), ((sib - 1) % N, "prv")])
+        for k, (d, buf) in enumerate(pairs):
+            rounds[4].append(move(sib, d, buf, near[k * w:k * w + w], near[h + k * w:h + k * w + w]))
+        if s in shared:
+            rounds[5].append((sib, near, near, ("prv_in",) * 2, "own", 0, "prv", 0, len(away) * CAPP))
+        return rounds
+
+    due = {}
+    for s in range(N):
+        for moves in plan(s):
+            for m in moves:
+                if m[0] == rank:
+                    for k in (0, 1):
+                        due[m[3][k]] = due.get(m[3][k], 0) + len(m[1 + k])
+    rounds = plan(rank)
+    sent = [0]
 
     def bits(es):
         m = 0
@@ -70,124 +123,98 @@ def rank_program(g, core, T, topo):
             m |= 1 << e
         return m
 
-    EA, EB, EF = 2, 1, 2
-
-    def transfer(dst, es, sem, src, out):
-        rid, pid = topo.addr(cores[dst])[:2]
-        return RemoteDMATransfer(dst_ids=[DstId(rid=rid, pnc=pid)], dma_engine_mask=bits(es), remote_sem=sem,
-                                 src=src, dst=out)
-
-    def both(moves, slot):
-        for kind in ("_c", "_s"):
+    def issue(moves, kinds=(0, 1)):
+        for k in kinds:
             ts = []
-            for dst, es, sem, a, i, b, j, w in moves:
-                src, out = T[a + kind][:, i:i + w], T[b + kind][:, j:j + w]
-                if kind == "_c":
+            for m in moves:
+                dst, es, sem, (a, i, b, j, w) = m[0], m[1 + k], m[3][k], m[4:]
+                src, out = T[a + ("_c", "_s")[k]][:, i:i + w], T[b + ("_c", "_s")[k]][:, j:j + w]
+                if k == 0:
                     src, out = src.bitcast(dt.uint8), out.bitcast(dt.uint8)
-                ts.append(transfer(dst, es, sem, src, out))
+                rid, pid = topo.addr(cores[dst])[:2]
+                ts.append(RemoteDMATransfer(dst_ids=[DstId(rid=rid, pnc=pid)], dma_engine_mask=bits(es),
+                                            remote_sem=M[sem], src=src, dst=out))
+                sent[0] += len(es)
             g.remote_dma_fused(ts, local_sem=M.sent)
-        return 2 * sum(len(m[1]) for m in moves)
-
-    def at(d):
-        return (shared if d in shared else rest).index(d) * CAPP
 
     for k in range(5):
         S.dma_start(T.lsend[16 * k:16 * k + 16, :], T.send[:]).then_inc(M.ld_send, 16)
     for k in range(5, 8):
         Y.dma_start(T.lsend[16 * k:16 * k + 16, :], T.send[:]).then_inc(M.ld_send, 16)
     Y.dma_start(T.xs[:], T.x[:]).then_inc(M.ld_x, 16)
-    g.dma_start(T.lmine[0:16, :], T.mine[:]).then_inc(M.ld_g, 16)
+    g.dma_start(T.lists[0:16, 0:L16], T.mine[:]).then_inc(M.ld_g, 16)
     for k in range(1, 8):
-        Y.dma_start(T.lmine[16 * k:16 * k + 16, :], T.mine[:]).then_inc(M.ld_mine, 16)
+        Y.dma_start(T.lists[16 * k:16 * k + 16, 0:L16], T.mine[:]).then_inc(M.ld_lists, 16)
     for k in range(8):
-        Y.dma_start(T.lprev[16 * k:16 * k + 16, :], T.prev[:]).then_inc(M.ld_prev, 16)
+        Y.dma_start(T.lists[16 * k:16 * k + 16, L16:2 * L16], T.prev[:]).then_inc(M.ld_lists, 16)
     g.iota(T.places[:], [[1, NT]], 0, 0, allow_small_or_imprecise_dtypes=True).then_inc(M.iot, 1)
     g.iota(T.pcol[:], [[0, 4]], 0, 1, allow_small_or_imprecise_dtypes=True).then_inc(M.iot, 1)
+    for k in (0, 1):
+        V.memset(T["h%d" % k][:, 4 * NBUCK[k] * CAPP:4 * WIDTH[k]], 0.0).then_inc(M.zero, 1)
     V.memset(T.inv[:], SKIP).then_inc(M.inv0, 1)
 
     V.wait_ge(M.ld_send, 128)
-    for buf, sem, first in (("offa", M.cva, shared[0]), ("offb", M.cvb, rest[0])):
-        for w in range(W16):
-            V.tensor_scalar(T[buf][:, w:HALF // 16:W16], T.lsend[:, W16 * first + w:N * W16:2 * W16], 0, 4,
-                            AluOpType.max, AluOpType.mult).then_inc(sem, 1)
+    conv = [0, 0, 0]
 
-    def gather(eng, tile, offs, t, sem):
-        win = T.xs[:, t:4 * NT].indirect(T[offs][:, 0:HALF // 16])
+    def offsets(k, out, src):
+        V.tensor_scalar(out, src, 0, 4, AluOpType.max, AluOpType.mult).then_inc(M["cv%d" % k], 1)
+        conv[k] += 1
+
+    for k, ds in enumerate(tiles(rank)):
+        for i, d in enumerate(ds):
+            if d in shared:
+                offsets(k, T["off%d" % k][:, W16 * i:W16 * i + W16], T.lsend[:, W16 * d:W16 * d + W16])
+    for w in range(W16):
+        offsets(2, T.off2[:, W16 + w::W16], T.lsend[:, W16 * rest[0] + w::2 * W16])
+
+    def copy(eng, out, src, sem):
         if eng is V:
-            V.tensor_copy(T[tile][:, t:4 * HALF:4], win).then_inc(sem, 1)
+            V.tensor_copy(out, src).then_inc(sem, 1)
         else:
-            S.activation(T[tile][:, t:4 * HALF:4], win, COPY).then_inc(sem, 1)
+            S.activation(out, src, COPY).then_inc(sem, 1)
 
-    for eng in (V, S):
-        eng.wait_ge(M.ld_x, 16)
-        eng.wait_ge(M.cva, W16)
-    for eng, t in ((V, 0), (S, 2), (V, 1), (S, 3)):
-        gather(eng, "ha", "offa", t, M.ga)
-    for eng in (V, S):
-        eng.wait_ge(M.cvb, W16)
-    for t in (2, 3):
-        gather(S, "hb", "offb", t, M.gb)
-    V.wait_ge(M.ga, 4)
-    V.quantize_mx(T.qa_c[:], T.qa_s[:], T.ha[:]).then_inc(M.qa, 1)
-    for t in (0, 1):
-        gather(V, "hb", "offb", t, M.gb)
-    V.wait_ge(M.gb, 4)
-    V.quantize_mx(T.qb_c[:], T.qb_s[:], T.hb[:]).then_inc(M.qb, 1)
+    V.wait_ge(M.zero, 2)
+    V.wait_ge(M.ld_x, 16)
+    S.wait_ge(M.ld_x, 16)
+    for k in range(3):
+        n = 4 * NBUCK[k] * CAPP
+        for eng, ts in ((V, (0, 1)), (S, (2, 3))):
+            eng.wait_ge(M["cv%d" % k], conv[k])
+            for t in ts:
+                copy(eng, T["h%d" % k][:, t:n:4], T.xs[:, t:4 * NT].indirect(T["off%d" % k][:]), M["ga%d" % k])
+        V.wait_ge(M["ga%d" % k], 4)
+        V.quantize_mx(T["q%d_c" % k][:], T["q%d_s" % k][:], T["h%d" % k][:]).then_inc(M["q%d" % k], 1)
 
-    sent = 0
-    mine_sl = rank * CAPP
-    hops = []
-    for k, r in enumerate([r for r in away if r in shared]):
-        es = ([off[4], off[5]], [off[6], off[7]], [off[0], off[2]])[k]
-        hops.append((r, es, M.own_in, "qa", at(r), "own", mine_sl, CAPP))
-    b = rank if heads else before
-    hops.append((sib, [off[1], off[3]], M.prv_in if heads else M.own_in, "qa", at(b), "prv" if heads else "own",
-                 mine_sl, CAPP))
-    g.wait_ge(M.qa, 1)
-    sent += both(hops, mine_sl)
-    hops = []
-    lone = [off[0], off[1], off[2], off[3], off[4], off[6]]
-    for d in rest:
-        for r, sem, buf in ((d, M.own_in, "own"), ((d + 1) % N, M.prv_in, "prv")):
-            if chip[r] != here:
-                hops.append((r, [lone.pop(0)], sem, "qb", at(d), buf, mine_sl, CAPP))
-            elif r == sib:
-                hops.append((r, [off[5]], sem, "qb", at(d), buf, mine_sl, CAPP))
-    g.wait_ge(M.qb, 1)
-    sent += both(hops, mine_sl)
-
+    for k in range(3):
+        g.wait_ge(M["q%d" % k], 1)
+        issue(rounds[k])
+    issue(rounds[3])
+    issue(rounds[4])
     for d, buf in ((rank, "own"), (before, "prv")):
-        q, sem = ("qa", M.qa) if d in shared else ("qb", M.qb)
-        Y.wait_ge(sem, 1)
-        Y.dma_start(T[buf + "_c"][:, mine_sl:mine_sl + CAPP].bitcast(dt.uint8),
-                    T[q + "_c"][:, at(d):at(d) + CAPP].bitcast(dt.uint8)).then_inc(M.selfc, 16)
-        Y.dma_start(T[buf + "_s"][:, mine_sl:mine_sl + CAPP], T[q + "_s"][:, at(d):at(d) + CAPP]).then_inc(M.selfc, 16)
+        q, i = at(rank, d)
+        j = slot(rank, rank)
+        Y.wait_ge(M[q], 1)
+        Y.dma_start(T[buf + "_c"][:, j:j + CAPP].bitcast(dt.uint8),
+                    T[q + "_c"][:, i:i + CAPP].bitcast(dt.uint8)).then_inc(M.selfc, 16)
+        Y.dma_start(T[buf + "_s"][:, j:j + CAPP], T[q + "_s"][:, i:i + CAPP]).then_inc(M.selfc, 16)
+    if rounds[5]:
+        for k, sem in enumerate(("hand_c", "hand_s")):
+            g.wait_ge(M[sem], due[sem])
+            issue(rounds[5], (k,))
 
-    chips = sorted(set(chip[r] for r in away), key=lambda c: chip.index(c))
-    if heads:
-        own_n = 2 * EA * (len(away) + 1)
-        prv_n = 2 * EB * (len(away) + 1)
-    else:
-        own_n = 2 * EB * (len(away) + 1)
-        prv_n = 2 * EA + 2 * EF * len(chips)
-    if heads:
-        hops = []
-        for k, c in enumerate(chips):
-            j = chip.index(c) * CAPP
-            hops.append((sib, near[EF * k:EF * k + EF], M.prv_in, "own", j, "prv", j, 2 * CAPP))
-        g.wait_ge(M.own_in, own_n)
-        sent += both(hops, 0)
-
-    V.wait_ge(M.ld_mine, 112)
+    b = base(rank) * CAPP
+    V.wait_ge(M.ld_lists, 240)
     V.wait_ge(M.ld_g, 16)
-    V.tensor_copy(T.moff[:], T.lmine[:]).then_inc(M.mo, 1)
-    V.wait_ge(M.ld_prev, 128)
-    V.tensor_copy(T.poff[:], T.lprev[:]).then_inc(M.po, 1)
+    V.tensor_scalar(T.wrap[:], T.lists[:], b, ARR, AluOpType.is_lt, AluOpType.mult).then_inc(M.wr, 1)
     V.wait_ge(M.iot, 2)
     V.tensor_scalar(T.diag[:], T.places[:, 0:128], T.pcol[:, 0:1], None, AluOpType.is_equal).then_inc(M.dia, 1)
+    V.wait_ge(M.wr, 1)
+    V.tensor_tensor(T.turn[:], T.lists[:], T.wrap[:], AluOpType.add).then_inc(M.tu, 1)
+    V.wait_ge(M.tu, 1)
+    V.tensor_scalar(T.moff[:], T.turn[:], b, None, AluOpType.subtract).then_inc(M.mo, 1)
     V.wait_ge(M.mo, 1)
     V.wait_ge(M.inv0, 1)
-    V.tensor_copy(T.inv[:].indirect(T.moff[:]), T.places[:]).then_inc(M.invd, 1)
+    V.tensor_copy(T.inv[:].indirect(T.moff[:, 0:L16]), T.places[:]).then_inc(M.invd, 1)
     V.wait_ge(M.invd, 1)
     V.wait_ge(M.dia, 1)
     for t in range(NTILE):
@@ -200,47 +227,52 @@ def rank_program(g, core, T, topo):
     V.wait_ge(M.ixf, NTILE)
     V.tensor_copy(T.idx[:, 0:NTILE], T.idxf[:, 0:NTILE]).then_inc(M.ix, 1)
 
+    def product(t, side, a, b, k, sem):
+        P.matmul_mx(T.ps[:, 512 * k:512 * k + b - a], T.own_c[:, 128 * t:128 * t + 128],
+                    T.own_s[:, 128 * t:128 * t + 128], T[side + "_c"][:, a:b], T[side + "_s"][:, a:b],
+                    True, True).then_inc(sem, 1)
+
     P.wait_ge(M.selfc, 64)
-    P.wait_ge(M.own_in, own_n)
-    for side, b0, pe in (("own", 0, "peo"), ("prv", NTILE, "pep")):
-        if side == "prv":
-            P.wait_ge(M.prv_in, prv_n)
-        for t in range(NTILE):
-            c0 = 512 * (b0 + t)
-            P.matmul_mx(T.ps[:, c0:c0 + ARR], T.own_c[:, 128 * t:128 * t + 128], T.own_s[:, 128 * t:128 * t + 128],
-                        T[side + "_c"][:], T[side + "_s"][:], True, True).then_inc(M[pe + str(t)], 1)
+    for sem in ("hand_c", "hand_s", "own_in"):
+        if sem in due:
+            P.wait_ge(M[sem], due[sem])
+    for t in range(NTILE):
+        product(t, "own", 0, ARR, t, M["peo%d" % t])
+    P.wait_ge(M.prv_in, due["prv_in"])
+    product(0, "prv", 0, ARR // 2, NTILE, M.pep0)
+    product(0, "prv", ARR // 2, ARR, 2 * NTILE, M.pepx)
+    for t in range(1, NTILE):
+        product(t, "prv", 0, ARR, NTILE + t, M["pep%d" % t])
 
-    def leave(eng, t, h):
-        c0 = 512 * (h * NTILE + t)
-        out, src, sem = T["raw%d" % t][:, h * ARR:h * ARR + ARR], T.ps[:, c0:c0 + ARR], M["ev%s%d" % ("op"[h], t)]
-        eng.wait_ge(M["pe%s%d" % ("op"[h], t)], 1)
-        if eng is V:
-            V.tensor_copy(out, src).then_inc(sem, 1)
-        else:
-            S.activation(out, src, COPY).then_inc(sem, 1)
+    def leave(eng, t, h, a, b, k, pe):
+        eng.wait_ge(pe, 1)
+        copy(eng, T["raw%d" % t][:, h * ARR + a:h * ARR + b], T.ps[:, 512 * k:512 * k + b - a],
+             M["ev%s%d" % ("op"[h], t)])
 
-    def order(eng, t, h):
-        win = T["raw%d" % t][:, h * ARR:h * ARR + ARR].indirect(T[("moff", "poff")[h]][:])
-        out = T["row%d" % t][:, h * NT:h * NT + NT]
-        eng.wait_ge(M["ev%s%d" % ("op"[h], t)], 1)
-        if eng is V:
-            V.tensor_copy(out, win).then_inc(M["rw%d" % t], 1)
-        else:
-            S.activation(out, win, COPY).then_inc(M["rw%d" % t], 1)
+    def order(eng, t, h, a, b, n):
+        eng.wait_ge(M["ev%s%d" % ("op"[h], t)], n)
+        win = T["raw%d" % t][:, h * ARR:h * ARR + ARR].indirect(T.moff[:, h * L16 + a // 16:h * L16 + b // 16])
+        copy(eng, T["row%d" % t][:, h * NT + a:h * NT + b], win, M["rw%d" % t])
 
-    V.wait_ge(M.po, 1)
     S.wait_ge(M.mo, 1)
-    S.wait_ge(M.po, 1)
-    leave(V, 0, 0), leave(V, 2, 0), order(V, 0, 0), order(V, 2, 0)
-    leave(S, 1, 0), order(S, 1, 0)
-    leave(V, 0, 1), order(V, 0, 1), leave(V, 2, 1), order(V, 2, 1)
-    leave(S, 1, 1), order(S, 1, 1)
+    for eng, ts in ((V, (0, 2)), (S, (1,))):
+        for t in ts:
+            leave(eng, t, 0, 0, ARR, t, M["peo%d" % t])
+        for t in ts:
+            order(eng, t, 0, 0, NT, 1)
+    leave(V, 0, 1, 0, ARR // 2, NTILE, M.pep0)
+    leave(S, 0, 1, ARR // 2, ARR, 2 * NTILE, M.pepx)
+    order(V, 0, 1, 0, NT // 2, 2)
+    order(S, 0, 1, NT // 2, NT, 2)
+    for eng, t in ((S, 1), (V, 2)):
+        leave(eng, t, 1, 0, ARR, NTILE + t, M["pep%d" % t])
+        order(eng, t, 1, 0, NT, 1)
 
     g.wait_ge(M.ix, 1)
     for t in range(NTILE):
-        g.wait_ge(M["rw%d" % t], 2)
+        g.wait_ge(M["rw%d" % t], 2 if t else 3)
         g.indirect_dma_start(T.y[:], IndirectOffsetOnAxis(ap=T.idx[:, t:t + 1], axis=0), T["row%d" % t][:], None,
                              bounds_check=NT - 1, oob_is_err=False).then_inc(M["st%d" % t], 16)
-    g.wait_ge(M.sent, sent)
+    g.wait_ge(M.sent, sent[0])
     for t in range(NTILE):
         g.wait_ge(M["st%d" % t], 16)

from concourse.bass import DstId, RemoteDMATransfer, IndirectOffsetOnAxis
from concourse.mybir import dt, AluOpType, AxisListType, ActivationFunctionType

N, NT, CAPP = 8, 256, 48
ARR = N * CAPP
NBUCK = (1, 2, 5)
WIDTH = (128, 128, 240)
W16 = CAPP // 16
L16 = NT // 16
NTILE = ARR // 128
SKIP = 1000.0

SCRATCH = {
    "xs": ("sbuf", [128, 4 * NT], "bfloat16"),
    "lsend": ("sbuf", [128, N * W16], "int32"),
    "lists": ("sbuf", [128, 2 * L16], "int32"),
    "wrap": ("sbuf", [128, 2 * L16], "int32"),
    "turn": ("sbuf", [128, 2 * L16], "int32"),
    "moff": ("sbuf", [128, 2 * L16], "uint16"),
    "own_c": ("sbuf", [128, ARR], "float8_e4m3fn_x4"),
    "own_s": ("sbuf", [128, ARR], "uint8"),
    "prv_c": ("sbuf", [128, ARR], "float8_e4m3fn_x4"),
    "prv_s": ("sbuf", [128, ARR], "uint8"),
    "places": ("sbuf", [128, NT], "float32"),
    "pcol": ("sbuf", [128, 4], "float32"),
    "diag": ("sbuf", [128, 128], "float32"),
    "inv": ("sbuf", [128, ARR], "float32"),
    "pick": ("sbuf", [128, ARR], "float32"),
    "idxf": ("sbuf", [128, 4], "float32"),
    "idx": ("sbuf", [128, 4], "int32"),
    "ps": ("psum", [128, 512 * (2 * NTILE + 1)], "float32"),
}
SEMAPHORES = ["ld_send", "ld_x", "ld_lists", "ld_g", "iot", "inv0", "zero", "selfc", "hand_c", "hand_s", "own_in",
              "prv_in", "sent", "wr", "tu", "mo", "invd", "dia", "pk", "ixf", "ix", "pepx"]
for _t in range(3):
    SCRATCH["off%d" % _t] = ("sbuf", [128, NBUCK[_t] * W16], "uint16")
    SCRATCH["h%d" % _t] = ("sbuf", [128, 4 * WIDTH[_t]], "bfloat16")
    SCRATCH["q%d_c" % _t] = ("sbuf", [128, WIDTH[_t]], "float8_e4m3fn_x4")
    SCRATCH["q%d_s" % _t] = ("sbuf", [128, WIDTH[_t]], "uint8")
    SEMAPHORES += ["cv%d" % _t, "ga%d" % _t, "q%d" % _t]
for _t in range(NTILE):
    SCRATCH["raw%d" % _t] = ("sbuf", [128, 2 * ARR], "float32")
    SCRATCH["row%d" % _t] = ("sbuf", [128, 2 * NT], "float32")
    SEMAPHORES += ["peo%d" % _t, "pep%d" % _t, "evo%d" % _t, "evp%d" % _t, "rw%d" % _t, "st%d" % _t]


def rank_program(g, core, T, topo):
    rank = T.rank_of(core)
    if rank is None:
        return
    V, S, Y, P, M = g.vector, g.scalar, g.sync, g.tensor, T.sem
    COPY = ActivationFunctionType.Copy
    cores = list(T.cores)
    chip = [topo.chip(c) for c in cores]
    shared = [d for d in range(N) if chip[d] == chip[(d + 1) % N]]
    rest = [d for d in range(N) if d not in shared]
    before = (rank - 1) % N

    def head(r):
        return r if r in shared else r - 1

    def tiles(s):
        a = sorted([d for d in shared if chip[d] != chip[s]], key=lambda d: (d - s) % N)
        return a[:1], a[1:], [head(s)] + rest

    def at(s, d):
        for k, ds in enumerate(tiles(s)):
            if d in ds:
                return "q%d" % k, ds.index(d) * CAPP

    def base(r):
        return (head(r) + 2) % N

    def slot(r, s):
        return (s - base(r)) % N * CAPP

    def plan(s):
        away = [r for r in range(N) if chip[r] != chip[s]]
        sib = [r for r in range(N) if r != s and chip[r] == chip[s]][0]
        off = topo.engines(cores[s], cores[away[0]])
        near = [e for e in topo.engines(cores[s], cores[sib]) if e not in off]
        q = len(off) // 4
        G = [off[q * k:q * k + q] for k in range(4)]

        def deal(a, b, c, d):
            return [G[c], G[d], G[a] + G[b]]

        def move(r, d, buf, es, fs, sems=None):
            return (r, es, fs, sems or (buf + "_in",) * 2) + at(s, d) + (buf, slot(r, s), CAPP)

        hand = ("hand_c", "hand_s")
        a0, a1, _ = tiles(s)
        rounds = [[move(a0[0], a0[0], "own", off, off, hand)],
                  [move(a1[0], a1[0], "own", G[0] + G[1], G[2] + G[3], hand),
                   move(a1[1], a1[1], "own", G[2] + G[3], G[0] + G[1], hand)], [], [], [], []]
        for k, step, buf, es, fs in ((2, 0, "own", deal(0, 1, 2, 3), deal(2, 3, 0, 1)),
                                     (3, 1, "prv", deal(2, 3, 0, 1), deal(0, 1, 2, 3))):
            for d in rest:
                r = (d + step) % N
                if r in away:
                    rounds[k].append(move(r, d, buf, es.pop(0), fs.pop(0)))
        w, h = len(near) // 4, len(near) // 2
        pairs = ([(s, "prv"), (sib, "own")] if s in shared else [(sib, "own"), ((sib - 1) % N, "prv")])
        for k, (d, buf) in enumerate(pairs):
            rounds[4].append(move(sib, d, buf, near[k * w:k * w + w], near[h + k * w:h + k * w + w]))
        if s in shared:
            rounds[5].append((sib, near, near, ("prv_in",) * 2, "own", 0, "prv", 0, len(away) * CAPP))
        return rounds

    due = {}
    for s in range(N):
        for moves in plan(s):
            for m in moves:
                if m[0] == rank:
                    for k in (0, 1):
                        due[m[3][k]] = due.get(m[3][k], 0) + len(m[1 + k])
    rounds = plan(rank)
    sent = [0]

    def bits(es):
        m = 0
        for e in es:
            m |= 1 << e
        return m

    def issue(moves, kinds=(0, 1)):
        for k in kinds:
            ts = []
            for m in moves:
                dst, es, sem, (a, i, b, j, w) = m[0], m[1 + k], m[3][k], m[4:]
                src, out = T[a + ("_c", "_s")[k]][:, i:i + w], T[b + ("_c", "_s")[k]][:, j:j + w]
                if k == 0:
                    src, out = src.bitcast(dt.uint8), out.bitcast(dt.uint8)
                rid, pid = topo.addr(cores[dst])[:2]
                ts.append(RemoteDMATransfer(dst_ids=[DstId(rid=rid, pnc=pid)], dma_engine_mask=bits(es),
                                            remote_sem=M[sem], src=src, dst=out))
                sent[0] += len(es)
            g.remote_dma_fused(ts, local_sem=M.sent)

    for k in range(5):
        S.dma_start(T.lsend[16 * k:16 * k + 16, :], T.send[:]).then_inc(M.ld_send, 16)
    for k in range(5, 8):
        Y.dma_start(T.lsend[16 * k:16 * k + 16, :], T.send[:]).then_inc(M.ld_send, 16)
    Y.dma_start(T.xs[:], T.x[:]).then_inc(M.ld_x, 16)
    g.dma_start(T.lists[0:16, 0:L16], T.mine[:]).then_inc(M.ld_g, 16)
    for k in range(1, 8):
        Y.dma_start(T.lists[16 * k:16 * k + 16, 0:L16], T.mine[:]).then_inc(M.ld_lists, 16)
    for k in range(8):
        Y.dma_start(T.lists[16 * k:16 * k + 16, L16:2 * L16], T.prev[:]).then_inc(M.ld_lists, 16)
    g.iota(T.places[:], [[1, NT]], 0, 0, allow_small_or_imprecise_dtypes=True).then_inc(M.iot, 1)
    g.iota(T.pcol[:], [[0, 4]], 0, 1, allow_small_or_imprecise_dtypes=True).then_inc(M.iot, 1)
    for k in (0, 1):
        V.memset(T["h%d" % k][:, 4 * NBUCK[k] * CAPP:4 * WIDTH[k]], 0.0).then_inc(M.zero, 1)
    V.memset(T.inv[:], SKIP).then_inc(M.inv0, 1)

    V.wait_ge(M.ld_send, 128)
    conv = [0, 0, 0]

    def offsets(k, out, src):
        V.tensor_scalar(out, src, 0, 4, AluOpType.max, AluOpType.mult).then_inc(M["cv%d" % k], 1)
        conv[k] += 1

    for k, ds in enumerate(tiles(rank)):
        for i, d in enumerate(ds):
            if d in shared:
                offsets(k, T["off%d" % k][:, W16 * i:W16 * i + W16], T.lsend[:, W16 * d:W16 * d + W16])
    for w in range(W16):
        offsets(2, T.off2[:, W16 + w::W16], T.lsend[:, W16 * rest[0] + w::2 * W16])

    def copy(eng, out, src, sem):
        if eng is V:
            V.tensor_copy(out, src).then_inc(sem, 1)
        else:
            S.activation(out, src, COPY).then_inc(sem, 1)

    V.wait_ge(M.zero, 2)
    V.wait_ge(M.ld_x, 16)
    S.wait_ge(M.ld_x, 16)
    for k in range(3):
        n = 4 * NBUCK[k] * CAPP
        for eng, ts in ((V, (0, 1)), (S, (2, 3))):
            eng.wait_ge(M["cv%d" % k], conv[k])
            for t in ts:
                copy(eng, T["h%d" % k][:, t:n:4], T.xs[:, t:4 * NT].indirect(T["off%d" % k][:]), M["ga%d" % k])
        V.wait_ge(M["ga%d" % k], 4)
        V.quantize_mx(T["q%d_c" % k][:], T["q%d_s" % k][:], T["h%d" % k][:]).then_inc(M["q%d" % k], 1)

    for k in range(3):
        g.wait_ge(M["q%d" % k], 1)
        issue(rounds[k])
    issue(rounds[3])
    issue(rounds[4])
    for d, buf in ((rank, "own"), (before, "prv")):
        q, i = at(rank, d)
        j = slot(rank, rank)
        Y.wait_ge(M[q], 1)
        Y.dma_start(T[buf + "_c"][:, j:j + CAPP].bitcast(dt.uint8),
                    T[q + "_c"][:, i:i + CAPP].bitcast(dt.uint8)).then_inc(M.selfc, 16)
        Y.dma_start(T[buf + "_s"][:, j:j + CAPP], T[q + "_s"][:, i:i + CAPP]).then_inc(M.selfc, 16)
    if rounds[5]:
        for k, sem in enumerate(("hand_c", "hand_s")):
            g.wait_ge(M[sem], due[sem])
            issue(rounds[5], (k,))

    b = base(rank) * CAPP
    V.wait_ge(M.ld_lists, 240)
    V.wait_ge(M.ld_g, 16)
    V.tensor_scalar(T.wrap[:], T.lists[:], b, ARR, AluOpType.is_lt, AluOpType.mult).then_inc(M.wr, 1)
    V.wait_ge(M.iot, 2)
    V.tensor_scalar(T.diag[:], T.places[:, 0:128], T.pcol[:, 0:1], None, AluOpType.is_equal).then_inc(M.dia, 1)
    V.wait_ge(M.wr, 1)
    V.tensor_tensor(T.turn[:], T.lists[:], T.wrap[:], AluOpType.add).then_inc(M.tu, 1)
    V.wait_ge(M.tu, 1)
    V.tensor_scalar(T.moff[:], T.turn[:], b, None, AluOpType.subtract).then_inc(M.mo, 1)
    V.wait_ge(M.mo, 1)
    V.wait_ge(M.inv0, 1)
    V.tensor_copy(T.inv[:].indirect(T.moff[:, 0:L16]), T.places[:]).then_inc(M.invd, 1)
    V.wait_ge(M.invd, 1)
    V.wait_ge(M.dia, 1)
    for t in range(NTILE):
        V.tensor_tensor(T.pick[:, 128 * t:128 * t + 128], T.inv[:, 128 * t:128 * t + 128], T.diag[:],
                        AluOpType.mult).then_inc(M.pk, 1)
    V.wait_ge(M.pk, NTILE)
    for t in range(NTILE):
        V.tensor_reduce(T.idxf[:, t:t + 1], T.pick[:, 128 * t:128 * t + 128], AxisListType.X,
                        AluOpType.add).then_inc(M.ixf, 1)
    V.wait_ge(M.ixf, NTILE)
    V.tensor_copy(T.idx[:, 0:NTILE], T.idxf[:, 0:NTILE]).then_inc(M.ix, 1)

    def product(t, side, a, b, k, sem):
        P.matmul_mx(T.ps[:, 512 * k:512 * k + b - a], T.own_c[:, 128 * t:128 * t + 128],
                    T.own_s[:, 128 * t:128 * t + 128], T[side + "_c"][:, a:b], T[side + "_s"][:, a:b],
                    True, True).then_inc(sem, 1)

    P.wait_ge(M.selfc, 64)
    for sem in ("hand_c", "hand_s", "own_in"):
        if sem in due:
            P.wait_ge(M[sem], due[sem])
    for t in range(NTILE):
        product(t, "own", 0, ARR, t, M["peo%d" % t])
    P.wait_ge(M.prv_in, due["prv_in"])
    product(0, "prv", 0, ARR // 2, NTILE, M.pep0)
    product(0, "prv", ARR // 2, ARR, 2 * NTILE, M.pepx)
    for t in range(1, NTILE):
        product(t, "prv", 0, ARR, NTILE + t, M["pep%d" % t])

    def leave(eng, t, h, a, b, k, pe):
        eng.wait_ge(pe, 1)
        copy(eng, T["raw%d" % t][:, h * ARR + a:h * ARR + b], T.ps[:, 512 * k:512 * k + b - a],
             M["ev%s%d" % ("op"[h], t)])

    def order(eng, t, h, a, b, n):
        eng.wait_ge(M["ev%s%d" % ("op"[h], t)], n)
        win = T["raw%d" % t][:, h * ARR:h * ARR + ARR].indirect(T.moff[:, h * L16 + a // 16:h * L16 + b // 16])
        copy(eng, T["row%d" % t][:, h * NT + a:h * NT + b], win, M["rw%d" % t])

    S.wait_ge(M.mo, 1)
    for eng, ts in ((V, (0, 2)), (S, (1,))):
        for t in ts:
            leave(eng, t, 0, 0, ARR, t, M["peo%d" % t])
        for t in ts:
            order(eng, t, 0, 0, NT, 1)
    leave(V, 0, 1, 0, ARR // 2, NTILE, M.pep0)
    leave(S, 0, 1, ARR // 2, ARR, 2 * NTILE, M.pepx)
    order(V, 0, 1, 0, NT // 2, 2)
    order(S, 0, 1, NT // 2, NT, 2)
    for eng, t in ((S, 1), (V, 2)):
        leave(eng, t, 1, 0, ARR, NTILE + t, M["pep%d" % t])
        order(eng, t, 1, 0, NT, 1)

    g.wait_ge(M.ix, 1)
    for t in range(NTILE):
        g.wait_ge(M["rw%d" % t], 2 if t else 3)
        g.indirect_dma_start(T.y[:], IndirectOffsetOnAxis(ap=T.idx[:, t:t + 1], axis=0), T["row%d" % t][:], None,
                             bounds_check=NT - 1, oob_is_err=False).then_inc(M["st%d" % t], 16)
    g.wait_ge(M.sent, sent[0])
    for t in range(NTILE):
        g.wait_ge(M["st%d" % t], 16)
